import numpy as np
import ml_dtypes

BF16 = ml_dtypes.bfloat16


def bf(x):
    return np.asarray(x, np.float32).astype(BF16)


def f32(x):
    return np.asarray(x, np.float32)


def f64(x):
    return np.asarray(x).astype(np.float64)


def striped(idx):
    return np.tile(idx.reshape(-1, 16).T, (8, 1))


S, K, M, N, D, V = 2048, 128, 512, 512, 8, 64


def gelu_tanh(v):
    return 0.5 * v * (1.0 + np.tanh(np.sqrt(2.0 / np.pi) * (v + 0.044715 * v**3)))


def setup_inputs():
    return {"table": bf(np.random.standard_normal((K, S))), "w": bf(np.random.standard_normal((K, M)) / np.sqrt(K)), "b": f32(0.5 * np.random.standard_normal((M, 1))), "offs": striped(np.random.permutation(np.tile(np.arange(S), 2))[:N])}


def reference(table, w, b, offs):
    idx = offs[:16].T.reshape(-1)
    x = f64(table)[:, idx]
    y = f64(w).T @ x
    z = gelu_tanh(y + f64(b))
    return z.reshape(M, V, D).max(axis=2)

@@ -1,0 +1,53 @@
+import concourse.mybir as mybir
+
+BF16, F32, U16 = mybir.dt.bfloat16, mybir.dt.float32, mybir.dt.uint16
+GELU_TANH = mybir.ActivationFunctionType.Gelu_apprx_tanh
+
+P = 128
+S = 2048
+M = 512
+N = 512
+D = 8
+V = N // D
+M_BLOCKS = M // P
+
+FLOPS = 2 * P * M * N
+BYTES = N * P * 2 + P * M * 2 + M * 4 + P * (N // 16) * 2 + M * V * 4
+
+
+def tile_gather_matmul_kernel(tc, table, w, b, offs, out):
+    nc = tc.nc
+    with (
+        tc.tile_pool(name="held", bufs=1) as held,
+        tc.tile_pool(name="work", bufs=M_BLOCKS) as work,
+        tc.psum_pool(name="psum", bufs=M_BLOCKS) as psum,
+    ):
+        offsets = held.tile([P, N // 16], U16, name="offsets")
+        nc.sync.dma_start(offsets[:], offs)
+        nodes = held.tile([P, S], BF16, name="nodes")
+        nc.sync.dma_start(nodes[:], table)
+        weights = held.tile([P, M], BF16, name="weights")
+        nc.scalar.dma_start(weights[:], w)
+        bias = held.tile([P, M_BLOCKS], F32, name="bias")
+        with nc.allow_non_contiguous_dma(reason="one float32 to a partition, 512 in all"):
+            nc.scalar.dma_start(bias[:], b.rearrange("(a p) o -> p (a o)", p=P))
+
+        for a in range(M_BLOCKS):
+            y = psum.tile([P, N], F32, name="y")
+            nc.tensor.matmul(
+                y[:],
+                weights[:, a * P : (a + 1) * P],
+                nodes[:].indirect(offsets[:]),
+                start=True,
+                stop=True,
+            )
+            z = work.tile([P, N], F32, name="z")
+            nc.scalar.activation(z[:], y[:], GELU_TANH, bias=bias[:, a : a + 1])
+            pooled = work.tile([P, V], F32, name="pooled")
+            nc.vector.tensor_reduce(
+                pooled[:],
+                z[:].rearrange("p (v d) -> p v d", d=D),
+                axis=mybir.AxisListType.X,
+                op=mybir.AluOpType.max,
+            )
+            nc.sync.dma_start(out[a * P : (a + 1) * P, :], pooled[:])

@@ -9,7 +9,9 @@ M = 512
 N = 512
 D = 8
 V = N // D
-M_BLOCKS = M // P
+A = M // P
+LAST_BLOCK_PIECES = 2
+WARM_UPS = 4
 
 FLOPS = 2 * P * M * N
 BYTES = N * P * 2 + P * M * 2 + M * 4 + P * (N // 16) * 2 + M * V * 4
@@ -19,35 +21,50 @@ def tile_gather_matmul_kernel(tc, table, w, b, offs, out):
     nc = tc.nc
     with (
         tc.tile_pool(name="held", bufs=1) as held,
-        tc.tile_pool(name="work", bufs=M_BLOCKS) as work,
-        tc.psum_pool(name="psum", bufs=M_BLOCKS) as psum,
+        tc.tile_pool(name="work", bufs=A) as work,
+        tc.psum_pool(name="psum", bufs=A) as psum,
+        tc.psum_pool(name="spare", bufs=1) as spare,
     ):
         offsets = held.tile([P, N // 16], U16, name="offsets")
         nc.sync.dma_start(offsets[:], offs)
+        w_as_given = held.tile([P, M], BF16, name="w_as_given")
+        nc.scalar.dma_start(w_as_given[:], w)
         nodes = held.tile([P, S], BF16, name="nodes")
-        nc.sync.dma_start(nodes[:], table)
-        weights = held.tile([P, M], BF16, name="weights")
-        nc.scalar.dma_start(weights[:], w)
-        bias = held.tile([P, M_BLOCKS], F32, name="bias")
-        with nc.allow_non_contiguous_dma(reason="one float32 to a partition, 512 in all"):
-            nc.scalar.dma_start(bias[:], b.rearrange("(a p) o -> p (a o)", p=P))
+        nc.scalar.dma_start(nodes[:], table)
+        bias = held.tile([P, A], F32, name="bias")
+        nc.sync.dma_start(bias[:], b.rearrange("(p a) o -> p (a o)", a=A))
 
-        for a in range(M_BLOCKS):
-            y = psum.tile([P, N], F32, name="y")
-            nc.tensor.matmul(
-                y[:],
-                weights[:, a * P : (a + 1) * P],
-                nodes[:].indirect(offsets[:]),
-                start=True,
-                stop=True,
-            )
-            z = work.tile([P, N], F32, name="z")
-            nc.scalar.activation(z[:], y[:], GELU_TANH, bias=bias[:, a : a + 1])
+        zeros = held.tile([P, N], BF16, name="zeros")
+        nc.gpsimd.memset(zeros[:], 0.0)
+        unused_z = held.tile([P, 1], F32, name="unused_z")
+        nc.scalar.activation(unused_z[:], zeros[:, 0:1], GELU_TANH)
+        unused_y = spare.tile([P, N], F32, name="unused_y")
+        for i in range(WARM_UPS):
+            nc.tensor.matmul(unused_y[:], zeros[:, 0:P], zeros[:], start=True, stop=True)
+
+        weights = held.tile([P, A, P], BF16, name="weights")
+        nc.vector.tensor_copy(weights[:], w_as_given[:].rearrange("k (p a) -> k a p", a=A))
+
+        out_by_block = out.rearrange("(p a) v -> p a v", a=A)
+        for a in range(A):
+            pieces = LAST_BLOCK_PIECES if a == A - 1 else 1
+            width = N // pieces
             pooled = work.tile([P, V], F32, name="pooled")
-            nc.vector.tensor_reduce(
-                pooled[:],
-                z[:].rearrange("p (v d) -> p v d", d=D),
-                axis=mybir.AxisListType.X,
-                op=mybir.AluOpType.max,
-            )
-            nc.sync.dma_start(out[a * P : (a + 1) * P, :], pooled[:])
+            for h in range(pieces):
+                y = psum.tile([P, width], F32, name="y")
+                nc.tensor.matmul(
+                    y[:],
+                    weights[:, a, :],
+                    nodes[:].indirect(offsets[:, h * width // 16 : (h + 1) * width // 16]),
+                    start=True,
+                    stop=True,
+                )
+                z = work.tile([P, width], F32, name="z")
+                nc.scalar.activation(z[:], y[:], GELU_TANH, bias=bias[:, a : a + 1])
+                nc.vector.tensor_reduce(
+                    pooled[:, h * width // D : (h + 1) * width // D],
+                    z[:].rearrange("p (v d) -> p v d", d=D),
+                    axis=mybir.AxisListType.X,
+                    op=mybir.AluOpType.max,
+                )
+            nc.sync.dma_start(out_by_block[:, a, :], pooled[:])

@@ -10,8 +10,9 @@ N = 512
 D = 8
 V = N // D
 A = M // P
-LAST_BLOCK_PIECES = 2
+HALF = N // 2
 WARM_UPS = 4
+PSUM_SLOTS = 6
 
 FLOPS = 2 * P * M * N
 BYTES = N * P * 2 + P * M * 2 + M * 4 + P * (N // 16) * 2 + M * V * 4
@@ -22,7 +23,7 @@ def tile_gather_matmul_kernel(tc, table, w, b, offs, out):
     with (
         tc.tile_pool(name="held", bufs=1) as held,
         tc.tile_pool(name="work", bufs=A) as work,
-        tc.psum_pool(name="psum", bufs=A) as psum,
+        tc.psum_pool(name="psum", bufs=PSUM_SLOTS) as psum,
         tc.psum_pool(name="spare", bufs=1) as spare,
     ):
         offsets = held.tile([P, N // 16], U16, name="offsets")
@@ -47,22 +48,20 @@ def tile_gather_matmul_kernel(tc, table, w, b, offs, out):
 
         out_by_block = out.rearrange("(p a) v -> p a v", a=A)
         for a in range(A):
-            pieces = LAST_BLOCK_PIECES if a == A - 1 else 1
-            width = N // pieces
             pooled = work.tile([P, V], F32, name="pooled")
-            for h in range(pieces):
-                y = psum.tile([P, width], F32, name="y")
+            for first in range(0, N, HALF):
+                y = psum.tile([P, HALF], F32, name="y")
                 nc.tensor.matmul(
                     y[:],
                     weights[:, a, :],
-                    nodes[:].indirect(offsets[:, h * width // 16 : (h + 1) * width // 16]),
+                    nodes[:].indirect(offsets[:, first // 16 : (first + HALF) // 16]),
                     start=True,
                     stop=True,
                 )
-                z = work.tile([P, width], F32, name="z")
+                z = work.tile([P, HALF], F32, name="z")
                 nc.scalar.activation(z[:], y[:], GELU_TANH, bias=bias[:, a : a + 1])
                 nc.vector.tensor_reduce(
-                    pooled[:, h * width // D : (h + 1) * width // D],
+                    pooled[:, first // D : (first + HALF) // D],
                     z[:].rearrange("p (v d) -> p v d", d=D),
                     axis=mybir.AxisListType.X,
                     op=mybir.AluOpType.max,

@@ -13,6 +13,7 @@ A = M // P
 HALF = N // 2
 WARM_UPS = 4
 PSUM_SLOTS = 6
+PIECES = A * (N // HALF)
 
 FLOPS = 2 * P * M * N
 BYTES = N * P * 2 + P * M * 2 + M * 4 + P * (N // 16) * 2 + M * V * 4
@@ -22,7 +23,8 @@ def tile_gather_matmul_kernel(tc, table, w, b, offs, out):
     nc = tc.nc
     with (
         tc.tile_pool(name="held", bufs=1) as held,
-        tc.tile_pool(name="work", bufs=A) as work,
+        tc.tile_pool(name="blocks", bufs=A) as blocks,
+        tc.tile_pool(name="pieces", bufs=PIECES) as pieces,
         tc.psum_pool(name="psum", bufs=PSUM_SLOTS) as psum,
         tc.psum_pool(name="spare", bufs=1) as spare,
     ):
@@ -48,7 +50,7 @@ def tile_gather_matmul_kernel(tc, table, w, b, offs, out):
 
         out_by_block = out.rearrange("(p a) v -> p a v", a=A)
         for a in range(A):
-            pooled = work.tile([P, V], F32, name="pooled")
+            pooled = blocks.tile([P, V], F32, name="pooled")
             for first in range(0, N, HALF):
                 y = psum.tile([P, HALF], F32, name="y")
                 nc.tensor.matmul(
@@ -58,7 +60,7 @@ def tile_gather_matmul_kernel(tc, table, w, b, offs, out):
                     start=True,
                     stop=True,
                 )
-                z = work.tile([P, HALF], F32, name="z")
+                z = pieces.tile([P, HALF], F32, name="z")
                 nc.scalar.activation(z[:], y[:], GELU_TANH, bias=bias[:, a : a + 1])
                 nc.vector.tensor_reduce(
                     pooled[:, first // D : (first + HALF) // D],

@@ -10,10 +10,10 @@ N = 512
 D = 8
 V = N // D
 A = M // P
-HALF = N // 2
+QUARTER = N // 4
 WARM_UPS = 4
-PSUM_SLOTS = 6
-PIECES = A * (N // HALF)
+PSUM_SLOTS = 7
+PIECES = A * (N // QUARTER)
 
 FLOPS = 2 * P * M * N
 BYTES = N * P * 2 + P * M * 2 + M * 4 + P * (N // 16) * 2 + M * V * 4
@@ -51,19 +51,19 @@ def tile_gather_matmul_kernel(tc, table, w, b, offs, out):
         out_by_block = out.rearrange("(p a) v -> p a v", a=A)
         for a in range(A):
             pooled = blocks.tile([P, V], F32, name="pooled")
-            for first in range(0, N, HALF):
-                y = psum.tile([P, HALF], F32, name="y")
+            for first in range(0, N, QUARTER):
+                y = psum.tile([P, QUARTER], F32, name="y")
                 nc.tensor.matmul(
                     y[:],
                     weights[:, a, :],
-                    nodes[:].indirect(offsets[:, first // 16 : (first + HALF) // 16]),
+                    nodes[:].indirect(offsets[:, first // 16 : (first + QUARTER) // 16]),
                     start=True,
                     stop=True,
                 )
-                z = pieces.tile([P, HALF], F32, name="z")
+                z = pieces.tile([P, QUARTER], F32, name="z")
                 nc.scalar.activation(z[:], y[:], GELU_TANH, bias=bias[:, a : a + 1])
                 nc.vector.tensor_reduce(
-                    pooled[:, first // D : (first + HALF) // D],
+                    pooled[:, first // D : (first + QUARTER) // D],
                     z[:].rearrange("p (v d) -> p v d", d=D),
                     axis=mybir.AxisListType.X,
                     op=mybir.AluOpType.max,

@@ -33,9 +33,9 @@ def tile_gather_matmul_kernel(tc, table, w, b, offs, out):
         w_as_given = held.tile([P, M], BF16, name="w_as_given")
         nc.scalar.dma_start(w_as_given[:], w)
         nodes = held.tile([P, S], BF16, name="nodes")
-        nc.scalar.dma_start(nodes[:], table)
+        nc.sync.dma_start(nodes[:], table)
         bias = held.tile([P, A], F32, name="bias")
-        nc.sync.dma_start(bias[:], b.rearrange("(p a) o -> p (a o)", a=A))
+        nc.scalar.dma_start(bias[:], b.rearrange("(p a) o -> p (a o)", a=A))
 
         zeros = held.tile([P, N], BF16, name="zeros")
         nc.gpsimd.memset(zeros[:], 0.0)

@@ -45,8 +45,10 @@ def tile_gather_matmul_kernel(tc, table, w, b, offs, out):
         for i in range(WARM_UPS):
             nc.tensor.matmul(unused_y[:], zeros[:, 0:P], zeros[:], start=True, stop=True)
 
-        weights = held.tile([P, A, P], BF16, name="weights")
-        nc.vector.tensor_copy(weights[:], w_as_given[:].rearrange("k (p a) -> k a p", a=A))
+        w_by_block = w_as_given[:].rearrange("k (p a) -> k a p", a=A)
+        weights = [held.tile([P, P], BF16, name="weights%d" % a) for a in range(A)]
+        for a in range(A):
+            nc.vector.tensor_copy(weights[a][:], w_by_block[:, a, :])
 
         out_by_block = out.rearrange("(p a) v -> p a v", a=A)
         for a in range(A):
@@ -55,7 +57,7 @@ def tile_gather_matmul_kernel(tc, table, w, b, offs, out):
                 y = psum.tile([P, QUARTER], F32, name="y")
                 nc.tensor.matmul(
                     y[:],
-                    weights[:, a, :],
+                    weights[a][:],
                     nodes[:].indirect(offsets[:, first // 16 : (first + QUARTER) // 16]),
                     start=True,
                     stop=True,

@@ -28,12 +28,12 @@ def tile_gather_matmul_kernel(tc, table, w, b, offs, out):
         tc.psum_pool(name="psum", bufs=PSUM_SLOTS) as psum,
         tc.psum_pool(name="spare", bufs=1) as spare,
     ):
-        offsets = held.tile([P, N // 16], U16, name="offsets")
-        nc.sync.dma_start(offsets[:], offs)
-        w_as_given = held.tile([P, M], BF16, name="w_as_given")
-        nc.scalar.dma_start(w_as_given[:], w)
         nodes = held.tile([P, S], BF16, name="nodes")
         nc.sync.dma_start(nodes[:], table)
+        w_as_given = held.tile([P, M], BF16, name="w_as_given")
+        nc.scalar.dma_start(w_as_given[:], w)
+        offsets = held.tile([P, N // 16], U16, name="offsets")
+        nc.sync.dma_start(offsets[:], offs)
         bias = held.tile([P, A], F32, name="bias")
         nc.scalar.dma_start(bias[:], b.rearrange("(p a) o -> p (a o)", a=A))
 

import concourse.mybir as mybir

BF16, F32, U16 = mybir.dt.bfloat16, mybir.dt.float32, mybir.dt.uint16
GELU_TANH = mybir.ActivationFunctionType.Gelu_apprx_tanh

P = 128
S = 2048
M = 512
N = 512
D = 8
V = N // D
A = M // P
QUARTER = N // 4
WARM_UPS = 4
PSUM_SLOTS = 7
PIECES = A * (N // QUARTER)

FLOPS = 2 * P * M * N
BYTES = N * P * 2 + P * M * 2 + M * 4 + P * (N // 16) * 2 + M * V * 4


def tile_gather_matmul_kernel(tc, table, w, b, offs, out):
    nc = tc.nc
    with (
        tc.tile_pool(name="held", bufs=1) as held,
        tc.tile_pool(name="blocks", bufs=A) as blocks,
        tc.tile_pool(name="pieces", bufs=PIECES) as pieces,
        tc.psum_pool(name="psum", bufs=PSUM_SLOTS) as psum,
        tc.psum_pool(name="spare", bufs=1) as spare,
    ):
        nodes = held.tile([P, S], BF16, name="nodes")
        nc.sync.dma_start(nodes[:], table)
        w_as_given = held.tile([P, M], BF16, name="w_as_given")
        nc.scalar.dma_start(w_as_given[:], w)
        offsets = held.tile([P, N // 16], U16, name="offsets")
        nc.sync.dma_start(offsets[:], offs)
        bias = held.tile([P, A], F32, name="bias")
        nc.scalar.dma_start(bias[:], b.rearrange("(p a) o -> p (a o)", a=A))

        zeros = held.tile([P, N], BF16, name="zeros")
        nc.gpsimd.memset(zeros[:], 0.0)
        unused_z = held.tile([P, 1], F32, name="unused_z")
        nc.scalar.activation(unused_z[:], zeros[:, 0:1], GELU_TANH)
        unused_y = spare.tile([P, N], F32, name="unused_y")
        for i in range(WARM_UPS):
            nc.tensor.matmul(unused_y[:], zeros[:, 0:P], zeros[:], start=True, stop=True)

        w_by_block = w_as_given[:].rearrange("k (p a) -> k a p", a=A)
        weights = [held.tile([P, P], BF16, name="weights%d" % a) for a in range(A)]
        for a in range(A):
            nc.vector.tensor_copy(weights[a][:], w_by_block[:, a, :])

        out_by_block = out.rearrange("(p a) v -> p a v", a=A)
        for a in range(A):
            pooled = blocks.tile([P, V], F32, name="pooled")
            for first in range(0, N, QUARTER):
                y = psum.tile([P, QUARTER], F32, name="y")
                nc.tensor.matmul(
                    y[:],
                    weights[a][:],
                    nodes[:].indirect(offsets[:, first // 16 : (first + QUARTER) // 16]),
                    start=True,
                    stop=True,
                )
                z = pieces.tile([P, QUARTER], F32, name="z")
                nc.scalar.activation(z[:], y[:], GELU_TANH, bias=bias[:, a : a + 1])
                nc.vector.tensor_reduce(
                    pooled[:, first // D : (first + QUARTER) // D],
                    z[:].rearrange("p (v d) -> p v d", d=D),
                    axis=mybir.AxisListType.X,
                    op=mybir.AluOpType.max,
                )
            nc.sync.dma_start(out_by_block[:, a, :], pooled[:])
